import numpy as np, ml_dtypes
CORES = [35,38,43,46]
N = 4
import mx_ref
BF = ml_dtypes.bfloat16
def entries(a):
    return np.ascontiguousarray(a.T).reshape(-1)
def table(e):
    return np.ascontiguousarray(np.reshape(e, (-1, 16)).T).astype(np.int32)
def cols(t, e):
    v = np.concatenate([t.reshape(128, -1, 4), np.zeros((128, 1, 4), BF)], axis=1)
    return np.ascontiguousarray(v[:, e]).reshape(128, -1)
def cut(t, i, w=512):
    return t[:, w * i:w * i + w]
def f(rng, *shape):
    return mx_ref.flush((rng.standard_normal(shape, dtype=np.float32) * np.exp2(rng.integers(-2, 3, shape[:-1] + (1,)))).astype(BF))
def wide(rng, *shape, cols=0):
    v = rng.standard_normal(shape, dtype=np.float32) * np.exp2(rng.integers(-12, 13, shape)).astype(np.float32)
    if cols: v *= np.repeat(np.exp2(rng.integers(-cols, cols + 1, shape[:-2] + (1, shape[-1] // 4))) * (rng.random(shape[:-2] + (1, shape[-1] // 4)) > 0.0625), 4, axis=-1).astype(np.float32)
    return mx_ref.flush(v.astype(BF))
T, K, O, CAPP = 512, 4, 4, 128
def lists(rng, foreign=False, own=False, same=False, absent=False):
    S = np.full((N, N, CAPP), -1); M = []
    for s in range(N):
        for d in range(N):
            n = CAPP if foreign else rng.integers(1, CAPP + 1)
            if s != d: S[s, d, rng.permutation(CAPP)[:n]] = rng.integers(0, T, n)
    k = np.arange(K)[:, None]
    for r in range(N):
        far = T + np.flatnonzero(S[:, r].reshape(-1) >= 0)
        m = np.where(rng.random((K, T)) < (1.0 if foreign else np.divide(k + 1, K + 1)), rng.choice(far, (K, T)), rng.integers(0, T, (K, T)))
        there = np.zeros((K, T), bool); there[rng.integers(0, K, T), np.arange(T)] = True
        if absent: there.reshape(-1)[rng.permutation(np.flatnonzero(~there))[:K * T - 2 * K * T // 3 - T]] = True
        else: there |= rng.random((K, T)) >= 0.1 + 0.5 * np.divide(k, K - 1)
        m = np.repeat(m[:, :1], T, axis=1) if same else np.where(there, m, -1)
        if own: m = np.stack([rng.permutation(T) for _ in range(K)])
        M.append(table(m))
    return {"send": np.stack([table(S[s]) for s in range(N)]), "mp": np.stack(M)}
def setup_inputs(rng):
    return {"x": f(rng, N, 128, 4 * T), "w": f(rng, N, 128, K * O * 512), **lists(rng)}
def setup_inputs_absent(rng):
    return {**setup_inputs(rng), **lists(rng, absent=True)}
def setup_inputs_foreign(rng):
    return {**setup_inputs(rng), **lists(rng, foreign=True)}
def setup_inputs_same(rng):
    return {**setup_inputs(rng), **lists(rng, same=True)}
def setup_inputs_spread(rng):
    d = setup_inputs(rng); d["x"] = wide(rng, N, 128, 4 * T); return d
def setup_inputs_own(rng):
    return {**setup_inputs(rng), **lists(rng, own=True)}
def check_inputs(d):
    b = []
    for n in ("x", "w"):
        a = np.abs(d[n].astype(np.float32))
        if not np.isfinite(a).all() or ((a > 0) & ((a < 2.0 ** -30) | (a > 2.0 ** 30))).any(): b.append(n)
    for r in range(N):
        s, m = entries(d["send"][r]), entries(d["mp"][r]).reshape(K, T)
        if s.min() < -1 or s.max() >= T or (s[r * CAPP:(r + 1) * CAPP] != -1).any(): b.append("send")
        held = np.concatenate([entries(d["send"][q])[r * CAPP:(r + 1) * CAPP] for q in range(N)])
        if m.min() < -1 or m.max() >= T + N * CAPP or (held[m[m >= T] - T] < 0).any() or (m < 0).all(axis=0).any(): b.append("mp")
    return b
def reference(x, w, send, mp):
    y = np.zeros((N, 128, O * T), np.float32)
    for r in range(N):
        held = [cols(x[s], entries(send[s])[r * CAPP:(r + 1) * CAPP]) for s in range(N)]
        v = np.concatenate([x[r]] + held, axis=1)
        m = entries(mp[r]).reshape(K, T)
        for k in range(K):
            q = mx_ref.quantize(cols(v, m[k]))
            for o in range(O): y[r][:, T * o:T * o + T] += mx_ref.matmul(mx_ref.quantize(cut(w[r], k * O + o)), q)
    return {"y": y}

@@ -1,0 +1,213 @@
+from concourse.bass import DstId, RemoteDMATransfer
+from concourse.mybir import dt, AluOpType, ActivationFunctionType
+
+N, TC, K, O, CAP = 4, 512, 4, 4, 128
+FAR = (N - 1) * CAP
+WS = 1 + TC + FAR
+PIECES = [2] * 8
+PAIR = 2
+BANKS = 8
+LAST = [(0, 256), (256, 384), (384, 512)]
+
+SCRATCH = {
+    "xs": ("sbuf", [128, 4 * TC], "bfloat16"),
+    "wb": ("sbuf", [128, 512 * K * O], "bfloat16"),
+    "sl": ("sbuf", [128, N * CAP // 16], "int32"),
+    "ml": ("sbuf", [128, K * TC // 16], "int32"),
+    "mt": ("sbuf", [128, K * TC // 16], "int32"),
+    "mu": ("sbuf", [128, K * TC // 16], "int32"),
+    "so": ("sbuf", [128, FAR // 16], "uint16"),
+    "mo": ("sbuf", [128, K * TC // 16], "uint16"),
+    "h": ("sbuf", [128, 4 * FAR], "bfloat16"),
+    "hq": ("sbuf", [128, FAR], "float8_e4m3fn_x4"),
+    "hs": ("sbuf", [128, FAR], "uint8"),
+    "xq": ("sbuf", [128, TC], "float8_e4m3fn_x4"),
+    "xp": ("sbuf", [128, TC], "uint8"),
+    "wq": ("sbuf", [128, 128 * K * O], "float8_e4m3fn_x4"),
+    "wp": ("sbuf", [128, 128 * K * O], "uint8"),
+    "fq": ("sbuf", [128, FAR], "float8_e4m3fn_x4"),
+    "fp": ("sbuf", [128, FAR], "uint8"),
+    "win": ("sbuf", [128, K * O * WS], "float32"),
+    "acc": ("sbuf", [128, O * TC], "float32"),
+    "ps": ("psum", [128, 512 * BANKS], "float32"),
+}
+SEMAPHORES = ["v", "s", "p", "arr", "loc", "lsl", "lml", "lx0", "lx1", "ly"] + ["lw%d" % i for i in range(len(PIECES))]
+
+VECTOR = """zero so qx0 h0 h2 qh ma qx1 mb qw0 mo qw1 qw2 E2 qw3 E4 qw4 E7 qw5 F4 F1 qw6 F5 G4 E10 G5 F7 F8 qw7
+    G6 G7 G8 G9 G12 G13 G10 G14 G11 G15a G15b G15c""".split()
+SCALAR = """h3 h1 E0 E1 E3 E5 E6 F0 I0 F2 I1 I2 F3 E8 F6 I3 E11 E9 F9 E12 F12 E13 F13 F10 F14 E14 F11 E15 F15""".split()
+TENSOR = """M0 M1 M2 M3 M4 M5 M6 M7 N0 N4 N1 N2 N5 M8 N3 M10 N7 N6 M9 M11 N8 M12 M13 M14 N9 M15
+    N12 N13 N10 N14 N11 N15""".split()
+
+
+def place(at, other):
+    return other if other < at else other - 1
+
+
+def engines_for(topo, cores, src, dst):
+    peers = [c for c in cores if c != src]
+    out = [c for c in peers if topo.chip(c) != topo.chip(src)]
+    if dst in out:
+        e = topo.engines(src, dst)
+        n = len(e) // len(out)
+        i = out.index(dst)
+        return e[i * n:(i + 1) * n]
+    used = {e for c in out for e in topo.engines(src, c)}
+    return [e for e in topo.engines(src, dst) if e not in used]
+
+
+def rank_program(g, core, T, topo):
+    r = T.rank_of(core)
+    if r is None:
+        return
+    cores = list(T.cores)
+    sem = T.sem
+    peers = [d for d in range(N) if d != r]
+    vec, act = g.vector, g.scalar
+    Copy = ActivationFunctionType.Copy
+    add = AluOpType.add
+    queue = {"v": g.vector, "s": g.scalar, "p": g.tensor, "y": g.sync, "g": g}
+    count = {"v": 0, "s": 0, "p": 0}
+    done = {}
+    waited = {}
+
+    def wait(q, token):
+        name, val = token
+        if waited.get((q, name), 0) < val:
+            queue[q].wait_ge(sem[name], val)
+            waited[(q, name)] = val
+
+    for b in range(8):
+        act.dma_start(T.sl[16 * b:16 * b + 16, :], T.send[:, :]).then_inc(sem.lsl, 16)
+    half = 2 * TC
+    for i in range(2):
+        g.sync.dma_start(T.xs[:, half * i:half * i + half], T.x[:, half * i:half * i + half]).then_inc(sem["lx%d" % i], 16)
+        done["x%d" % i] = ("lx%d" % i, 16)
+    for b in range(8):
+        g.sync.dma_start(T.ml[16 * b:16 * b + 16, :], T.mp[:, :]).then_inc(sem.lml, 16)
+    done["sl"], done["ml"] = ("lsl", 128), ("lml", 128)
+    piece, a = [], 0
+    for i, n in enumerate(PIECES):
+        g.sync.dma_start(T.wb[:, 512 * a:512 * (a + n)], T.w[:, 512 * a:512 * (a + n)]).then_inc(sem["lw%d" % i], 16)
+        done["w%d" % i] = ("lw%d" % i, 16)
+        piece += ["w%d" % i] * n
+        a += n
+
+    calls = {}
+    lw = CAP // 16
+
+    def slots(a, b, c):
+        return lambda: vec.tensor_scalar(T.so[:, a:b], T.sl[:, c:c + b - a], 4.0, 0.0, AluOpType.mult, AluOpType.max)
+
+    runs = [(0, lw * r, 0), (lw * r, lw * (N - 1), lw * (r + 1))]
+    calls["so"] = [(["sl"], slots(*x)) for x in runs if x[1] > x[0]]
+    calls["zero"] = [([], lambda: vec.memset(T.win[:, 0:K * O * WS:WS], 0.0))]
+    edge = float(TC + CAP * (r + 1))
+    if r == N - 1:
+        calls["ma"], calls["mb"] = [], []
+        done["ma"] = done["mb"] = done["ml"]
+        calls["mo"] = [(["ml"], lambda: vec.tensor_scalar(T.mo[:], T.ml[:], 1.0, None, add))]
+    else:
+        calls["ma"] = [(["ml"], lambda: vec.tensor_scalar(T.mt[:], T.ml[:], edge, -float(CAP), AluOpType.is_ge, AluOpType.mult))]
+        calls["mb"] = [(["ma"], lambda: vec.tensor_tensor(T.mu[:], T.mt[:], T.ml[:], add))]
+        calls["mo"] = [(["mb"], lambda: vec.tensor_scalar(T.mo[:], T.mu[:], 1.0, None, add))]
+
+    def copy(name, out, src):
+        if name in VECTOR:
+            return lambda: vec.tensor_copy(out, src)
+        return lambda: act.activation(out, src, Copy)
+
+    def quant(cq, cp, src, a, b):
+        return lambda: vec.quantize_mx(cq[:, a:b], cp[:, a:b], src[:, 4 * a:4 * b])
+
+    for t in range(4):
+        name = "h%d" % t
+        calls[name] = [(["so", "x0", "x1"], copy(name, T.h[:, t:4 * FAR:4], T.xs[:, t:4 * TC].indirect(T.so[:, 0:FAR // 16])))]
+    calls["qh"] = [(["h0", "h1", "h2", "h3"], quant(T.hq, T.hs, T.h, 0, FAR))]
+    for i in range(2):
+        calls["qx%d" % i] = [(["x%d" % i], quant(T.xq, T.xp, T.xs, TC // 2 * i, TC // 2 * (i + 1)))]
+    for i in range(K * O // PAIR):
+        a, b = PAIR * i, PAIR * (i + 1)
+        calls["qw%d" % i] = [(sorted(set(piece[a:b])), quant(T.wq, T.wp, T.wb, 128 * a, 128 * b))]
+
+    def product(i, q, p, n, bank):
+        w = slice(128 * i, 128 * i + 128)
+        return lambda: g.tensor.matmul_mx(T.ps[:, 512 * bank:512 * bank + n], T.wq[:, w], T.wp[:, w], q[:, 0:n], p[:, 0:n], True, True)
+
+    def out_of(name):
+        return {"M": "E", "N": "F"}[name[0]] + name[1:]
+
+    for j, name in enumerate(TENSOR):
+        far, i, bank = name[0] == "N", int(name[1:]), j % BANKS
+        n, e = (FAR if far else TC), out_of(name)
+        need = (["arr"] if far else ["qx0", "qx1"]) + ["qw%d" % (i // PAIR)] + ([out_of(TENSOR[j - BANKS])] if j >= BANKS else [])
+        calls[name] = [(need, product(i, T.fq if far else T.xq, T.fp if far else T.xp, n, bank))]
+        a = WS * i + 1 + (TC if far else 0)
+        calls[e] = [([name], copy(e, T.win[:, a:a + n], T.ps[:, 512 * bank:512 * bank + n]))]
+
+    def window(i, a, b):
+        m = i // O * (TC // 16)
+        return T.win[:, WS * i:WS * i + WS].indirect(T.mo[:, m + a // 16:m + b // 16])
+
+    def more(i, a, b):
+        at = T.acc[:, TC * (i % O) + a:TC * (i % O) + b]
+        return lambda: vec.tensor_tensor(at, window(i, a, b), at, add)
+
+    leave = []
+    for o in range(O):
+        calls["I%d" % o] = [(["zero", "mo", "E%d" % o, "F%d" % o], copy("I%d" % o, T.acc[:, TC * o:TC * o + TC], window(o, 0, TC)))]
+        last = "I%d" % o
+        for k in range(1, K):
+            i = k * O + o
+            need = ["zero", "mo", "E%d" % i, "F%d" % i, last]
+            last = "G%d" % i
+            parts = [(last, 0, TC)] if last in VECTOR else [(last + "abc"[j], a, b) for j, (a, b) in enumerate(LAST)]
+            for name, a, b in parts:
+                calls[name] = [(need, more(i, a, b))]
+        leave += [(name, TC * o + a, TC * o + b) for name, a, b in parts]
+    leave.sort(key=lambda x: VECTOR.index(x[0]))
+
+    width = {d: engines_for(topo, cores, core, cores[d]) for d in peers}
+    done["arr"] = ("arr", sum(2 * len(engines_for(topo, cores, cores[s], core)) for s in peers))
+
+    def send():
+        wait("g", done["qh"])
+        for codes in (True, False):
+            transfers = []
+            for d in peers:
+                rid, pid = topo.addr(cores[d])[:2]
+                a, b = CAP * place(r, d), CAP * place(d, r)
+                if codes:
+                    src, dst = T.hq[:, a:a + CAP].bitcast(dt.uint8), T.fq[:, b:b + CAP].bitcast(dt.uint8)
+                else:
+                    src, dst = T.hs[:, a:a + CAP], T.fp[:, b:b + CAP]
+                transfers.append(RemoteDMATransfer(dst_ids=[DstId(rid=rid, pnc=pid)], dma_engine_mask=sum(1 << e for e in width[d]),
+                                                   remote_sem=sem.arr, src=src, dst=dst))
+            g.remote_dma_fused(transfers, local_sem=sem.loc)
+
+    orders = {"v": list(VECTOR), "s": list(SCALAR), "p": list(TENSOR)}
+    moved = True
+    while moved:
+        moved = False
+        for q in orders:
+            while orders[q] and all(d in done or d == orders[q][0] for need, c in calls[orders[q][0]] for d in need):
+                name = orders[q].pop(0)
+                for need, call in calls[name]:
+                    for d in need:
+                        wait(q, done[d])
+                    call().then_inc(sem[q], 1)
+                    count[q] += 1
+                    done[name] = (q, count[q])
+                if name == "qh":
+                    send()
+                moved = True
+    if any(orders.values()):
+        raise ValueError("no order: %s" % orders)
+
+    for name, a, b in leave:
+        wait("y", done[name])
+        g.sync.dma_start(T.y[:, a:b], T.acc[:, a:b]).then_inc(sem.ly, 16)
+    g.wait_ge(sem.loc, 2 * sum(len(width[d]) for d in peers))
+    for q in orders:
+        wait("y", (q, count[q]))
+    g.sync.wait_ge(sem.ly, 16 * len(leave))

@@ -4,10 +4,11 @@ from concourse.mybir import dt, AluOpType, ActivationFunctionType
 N, TC, K, O, CAP = 4, 512, 4, 4, 128
 FAR = (N - 1) * CAP
 WS = 1 + TC + FAR
-PIECES = [2] * 8
 PAIR = 2
 BANKS = 8
 LAST = [(0, 256), (256, 384), (384, 512)]
+TILE = [(k, o) for h in range(0, O, PAIR) for k in range(K) for o in range(h, h + PAIR)]
+SLP, MLP = 32, 64
 
 SCRATCH = {
     "xs": ("sbuf", [128, 4 * TC], "bfloat16"),
@@ -31,13 +32,14 @@ SCRATCH = {
     "acc": ("sbuf", [128, O * TC], "float32"),
     "ps": ("psum", [128, 512 * BANKS], "float32"),
 }
-SEMAPHORES = ["v", "s", "p", "arr", "loc", "lsl", "lml", "lx0", "lx1", "ly"] + ["lw%d" % i for i in range(len(PIECES))]
+SEMAPHORES = ["v", "s", "p", "arr", "loc", "lsl", "lml", "lx0", "lx1", "ly"] + ["lw%d" % i for i in range(K * O // PAIR)]
 
-VECTOR = """zero so qx0 h0 h2 qh ma qx1 mb qw0 mo qw1 qw2 E2 qw3 E4 qw4 E7 qw5 F4 F1 qw6 F5 G4 E10 G5 F7 F8 qw7
-    G6 G7 G8 G9 G12 G13 G10 G14 G11 G15a G15b G15c""".split()
-SCALAR = """h3 h1 E0 E1 E3 E5 E6 F0 I0 F2 I1 I2 F3 E8 F6 I3 E11 E9 F9 E12 F12 E13 F13 F10 F14 E14 F11 E15 F15""".split()
-TENSOR = """M0 M1 M2 M3 M4 M5 M6 M7 N0 N4 N1 N2 N5 M8 N3 M10 N7 N6 M9 M11 N8 M12 M13 M14 N9 M15
-    N12 N13 N10 N14 N11 N15""".split()
+VECTOR = """zero so qx0 h0 qw0 qx1 ma qw1 mb qh qw2 qw3 E3 qw4 qw5 E7 qw6 E9 qw7 E11 mo E13 E15
+    F1 F2 F3 F5 G2 G3 G4 G5 G6 G10 G7 G12 G11 G14 G13 G15a G15b G15c""".split()
+SCALAR = """h1 h2 h3 E0 E1 E2 E4 E5 E6 E8 E10 E12 E14
+    F0 I0 I1 F4 F6 F8 I8 F10 F7 F12 F9 I9 F11 F14 F13 F15""".split()
+TENSOR = """M0 M1 M2 M3 M4 M5 M6 M7 M8 M9 M10 M11 M12 M13 M14 M15
+    N0 N1 N2 N3 N4 N5 N6 N8 N10 N7 N12 N9 N11 N14 N13 N15""".split()
 
 
 def place(at, other):
@@ -77,40 +79,43 @@ def rank_program(g, core, T, topo):
             queue[q].wait_ge(sem[name], val)
             waited[(q, name)] = val
 
-    for b in range(8):
-        act.dma_start(T.sl[16 * b:16 * b + 16, :], T.send[:, :]).then_inc(sem.lsl, 16)
+    for b, q in enumerate((act, g.sync)):
+        q.dma_start(T.sl[16 * b:16 * b + 16, :], T.send[:, :]).then_inc(sem.lsl, 16)
     half = 2 * TC
     for i in range(2):
         g.sync.dma_start(T.xs[:, half * i:half * i + half], T.x[:, half * i:half * i + half]).then_inc(sem["lx%d" % i], 16)
         done["x%d" % i] = ("lx%d" % i, 16)
-    for b in range(8):
-        g.sync.dma_start(T.ml[16 * b:16 * b + 16, :], T.mp[:, :]).then_inc(sem.lml, 16)
-    done["sl"], done["ml"] = ("lsl", 128), ("lml", 128)
-    piece, a = [], 0
-    for i, n in enumerate(PIECES):
-        g.sync.dma_start(T.wb[:, 512 * a:512 * (a + n)], T.w[:, 512 * a:512 * (a + n)]).then_inc(sem["lw%d" % i], 16)
+    for b in range(MLP // 16):
+        act.dma_start(T.ml[16 * b:16 * b + 16, :], T.mp[:, :]).then_inc(sem.lml, 16)
+    done["sl"], done["ml"] = ("lsl", SLP), ("lml", MLP)
+    for i in range(K * O // PAIR):
+        k, o = TILE[PAIR * i]
+        a, n = 512 * (k * O + o), 512 * PAIR
+        g.sync.dma_start(T.wb[:, n * i:n * i + n], T.w[:, a:a + n]).then_inc(sem["lw%d" % i], 16)
         done["w%d" % i] = ("lw%d" % i, 16)
-        piece += ["w%d" % i] * n
-        a += n
 
     calls = {}
     lw = CAP // 16
 
-    def slots(a, b, c):
-        return lambda: vec.tensor_scalar(T.so[:, a:b], T.sl[:, c:c + b - a], 4.0, 0.0, AluOpType.mult, AluOpType.max)
+    def slots(p, a, b, c):
+        return lambda: vec.tensor_scalar(T.so[p:p + SLP, a:b], T.sl[0:SLP, c:c + b - a], 4.0, 0.0, AluOpType.mult, AluOpType.max)
 
     runs = [(0, lw * r, 0), (lw * r, lw * (N - 1), lw * (r + 1))]
-    calls["so"] = [(["sl"], slots(*x)) for x in runs if x[1] > x[0]]
+    calls["so"] = [(["sl"], slots(p, *x)) for p in range(0, 128, SLP) for x in runs if x[1] > x[0]]
     calls["zero"] = [([], lambda: vec.memset(T.win[:, 0:K * O * WS:WS], 0.0))]
     edge = float(TC + CAP * (r + 1))
+
+    def maps(p, src):
+        return lambda: vec.tensor_scalar(T.mo[p:p + MLP, :], src[0:MLP, :], 1.0, None, add)
+
     if r == N - 1:
         calls["ma"], calls["mb"] = [], []
         done["ma"] = done["mb"] = done["ml"]
-        calls["mo"] = [(["ml"], lambda: vec.tensor_scalar(T.mo[:], T.ml[:], 1.0, None, add))]
+        calls["mo"] = [(["ml"], maps(p, T.ml)) for p in range(0, 128, MLP)]
     else:
-        calls["ma"] = [(["ml"], lambda: vec.tensor_scalar(T.mt[:], T.ml[:], edge, -float(CAP), AluOpType.is_ge, AluOpType.mult))]
-        calls["mb"] = [(["ma"], lambda: vec.tensor_tensor(T.mu[:], T.mt[:], T.ml[:], add))]
-        calls["mo"] = [(["mb"], lambda: vec.tensor_scalar(T.mo[:], T.mu[:], 1.0, None, add))]
+        calls["ma"] = [(["ml"], lambda: vec.tensor_scalar(T.mt[0:MLP, :], T.ml[0:MLP, :], edge, -float(CAP), AluOpType.is_ge, AluOpType.mult))]
+        calls["mb"] = [(["ma"], lambda: vec.tensor_tensor(T.mu[0:MLP, :], T.mt[0:MLP, :], T.ml[0:MLP, :], add))]
+        calls["mo"] = [(["mb"], maps(p, T.mu)) for p in range(0, 128, MLP)]
 
     def copy(name, out, src):
         if name in VECTOR:
@@ -127,8 +132,7 @@ def rank_program(g, core, T, topo):
     for i in range(2):
         calls["qx%d" % i] = [(["x%d" % i], quant(T.xq, T.xp, T.xs, TC // 2 * i, TC // 2 * (i + 1)))]
     for i in range(K * O // PAIR):
-        a, b = PAIR * i, PAIR * (i + 1)
-        calls["qw%d" % i] = [(sorted(set(piece[a:b])), quant(T.wq, T.wp, T.wb, 128 * a, 128 * b))]
+        calls["qw%d" % i] = [(["w%d" % i], quant(T.wq, T.wp, T.wb, 128 * PAIR * i, 128 * PAIR * (i + 1)))]
 
     def product(i, q, p, n, bank):
         w = slice(128 * i, 128 * i + 128)
@@ -146,19 +150,23 @@ def rank_program(g, core, T, topo):
         calls[e] = [([name], copy(e, T.win[:, a:a + n], T.ps[:, 512 * bank:512 * bank + n]))]
 
     def window(i, a, b):
-        m = i // O * (TC // 16)
+        m = TILE[i][0] * (TC // 16)
         return T.win[:, WS * i:WS * i + WS].indirect(T.mo[:, m + a // 16:m + b // 16])
 
     def more(i, a, b):
-        at = T.acc[:, TC * (i % O) + a:TC * (i % O) + b]
+        o = TILE[i][1]
+        at = T.acc[:, TC * o + a:TC * o + b]
         return lambda: vec.tensor_tensor(at, window(i, a, b), at, add)
 
     leave = []
     for o in range(O):
-        calls["I%d" % o] = [(["zero", "mo", "E%d" % o, "F%d" % o], copy("I%d" % o, T.acc[:, TC * o:TC * o + TC], window(o, 0, TC)))]
-        last = "I%d" % o
-        for k in range(1, K):
-            i = k * O + o
+        tiles = [i for i in range(K * O) if TILE[i][1] == o]
+        first = [i for i in tiles if "I%d" % i in SCALAR + VECTOR][0]
+        last = "I%d" % first
+        calls[last] = [(["zero", "mo", "E%d" % first, "F%d" % first], copy(last, T.acc[:, TC * o:TC * o + TC], window(first, 0, TC)))]
+        rest = [i for i in tiles if i != first]
+        rest.sort(key=lambda i: VECTOR.index("G%d" % i if "G%d" % i in VECTOR else "G%da" % i))
+        for i in rest:
             need = ["zero", "mo", "E%d" % i, "F%d" % i, last]
             last = "G%d" % i
             parts = [(last, 0, TC)] if last in VECTOR else [(last + "abc"[j], a, b) for j, (a, b) in enumerate(LAST)]

@@ -5,18 +5,25 @@ N, TC, K, O, CAP = 4, 512, 4, 4, 128
 FAR = (N - 1) * CAP
 WS = 1 + TC + FAR
 PAIR = 2
+PIECES = [1, 1] + [PAIR] * 7
 BANKS = 8
-LAST = [(0, 256), (256, 384), (384, 512)]
+LAST = [(0, 192), (192, 384), (384, 512)]
 TILE = [(k, o) for h in range(0, O, PAIR) for k in range(K) for o in range(h, h + PAIR)]
-SLP, MLP = 32, 64
+SUMS = [[0, 2], [4, 6], [1, 3], [5, 7], [8, 10, 12, 14], [9, 11, 13, 15]]
+TWICE = [o for o in range(O) if [TILE[s[0]][1] for s in SUMS].count(o) > 1]
+SLP = 32
+MP = 32
+MW = K * TC // MP
+NEAR = 4
 
 SCRATCH = {
     "xs": ("sbuf", [128, 4 * TC], "bfloat16"),
     "wb": ("sbuf", [128, 512 * K * O], "bfloat16"),
     "sl": ("sbuf", [128, N * CAP // 16], "int32"),
-    "ml": ("sbuf", [128, K * TC // 16], "int32"),
-    "mt": ("sbuf", [128, K * TC // 16], "int32"),
-    "mu": ("sbuf", [128, K * TC // 16], "int32"),
+    "ml": ("sbuf", [MP, MW], "int32"),
+    "mt": ("sbuf", [MP, MW], "int32"),
+    "mu": ("sbuf", [MP, MW], "int32"),
+    "mv": ("sbuf", [MP, MW], "uint16"),
     "so": ("sbuf", [128, FAR // 16], "uint16"),
     "mo": ("sbuf", [128, K * TC // 16], "uint16"),
     "h": ("sbuf", [128, 4 * FAR], "bfloat16"),
@@ -29,17 +36,17 @@ SCRATCH = {
     "fq": ("sbuf", [128, FAR], "float8_e4m3fn_x4"),
     "fp": ("sbuf", [128, FAR], "uint8"),
     "win": ("sbuf", [128, K * O * WS], "float32"),
-    "acc": ("sbuf", [128, O * TC], "float32"),
+    "acc": ("sbuf", [128, len(SUMS) * TC], "float32"),
     "ps": ("psum", [128, 512 * BANKS], "float32"),
 }
-SEMAPHORES = ["v", "s", "p", "arr", "loc", "lsl", "lml", "lx0", "lx1", "ly"] + ["lw%d" % i for i in range(K * O // PAIR)]
+SEMAPHORES = ["v", "s", "p", "arr", "loc", "lsl", "lml", "lmo", "lx0", "lx1", "lg"] + ["ly%d" % o for o in range(O)] + ["lw%d" % i for i in range(len(PIECES))]
 
-VECTOR = """zero so qx0 h0 qw0 qx1 ma qw1 mb qh qw2 qw3 E3 qw4 qw5 E7 qw6 E9 qw7 E11 mo E13 E15
-    F1 F2 F3 F5 G2 G3 G4 G5 G6 G10 G7 G12 G11 G14 G13 G15a G15b G15c""".split()
-SCALAR = """h1 h2 h3 E0 E1 E2 E4 E5 E6 E8 E10 E12 E14
-    F0 I0 I1 F4 F6 F8 I8 F10 F7 F12 F9 I9 F11 F14 F13 F15""".split()
-TENSOR = """M0 M1 M2 M3 M4 M5 M6 M7 M8 M9 M10 M11 M12 M13 M14 M15
-    N0 N1 N2 N3 N4 N5 N6 N8 N10 N7 N12 N9 N11 N14 N13 N15""".split()
+VECTOR = """zero so qx0 qx1 qw0 h0 qw1 h1a qw2 qha qhb qw3 ma qw4 mb qw5 mo E4 qw6 qw7 E7 qw8 E10 E12 E13
+    F0 F2 F3 F4 G2 F6 G3 F10 G6 F7 G10 G7 G12 G11 G14 G13 G15a G15b G15c""".split()
+SCALAR = """h2 h3 h1b E0 E1 E2 E3 E5 E6 E8 E9 E11 E14
+    F1 I0 I1 F8 I4 F5 I8 I5 F9 F12 F11 I9 F14 F13 F15 E15""".split()
+TENSOR = """M0 M1 M2 M3 M4 M5 M6 M7 M8 M9 M10 M11 M12 M13 M14
+    N0 N1 N2 N3 N4 N8 N6 N5 N10 N7 N9 N12 N11 N14 N13 N15 M15""".split()
 
 
 def place(at, other):
@@ -55,7 +62,8 @@ def engines_for(topo, cores, src, dst):
         i = out.index(dst)
         return e[i * n:(i + 1) * n]
     used = {e for c in out for e in topo.engines(src, c)}
-    return [e for e in topo.engines(src, dst) if e not in used]
+    free = [e for e in topo.engines(src, dst) if e not in used]
+    return free[::len(free) // NEAR]
 
 
 def rank_program(g, core, T, topo):
@@ -79,20 +87,21 @@ def rank_program(g, core, T, topo):
             queue[q].wait_ge(sem[name], val)
             waited[(q, name)] = val
 
-    for b, q in enumerate((act, g.sync)):
+    for b, q in enumerate((act, g.sync) * (SLP // 32)):
         q.dma_start(T.sl[16 * b:16 * b + 16, :], T.send[:, :]).then_inc(sem.lsl, 16)
     half = 2 * TC
     for i in range(2):
         g.sync.dma_start(T.xs[:, half * i:half * i + half], T.x[:, half * i:half * i + half]).then_inc(sem["lx%d" % i], 16)
         done["x%d" % i] = ("lx%d" % i, 16)
-    for b in range(MLP // 16):
-        act.dma_start(T.ml[16 * b:16 * b + 16, :], T.mp[:, :]).then_inc(sem.lml, 16)
-    done["sl"], done["ml"] = ("lsl", SLP), ("lml", MLP)
-    for i in range(K * O // PAIR):
-        k, o = TILE[PAIR * i]
-        a, n = 512 * (k * O + o), 512 * PAIR
-        g.sync.dma_start(T.wb[:, n * i:n * i + n], T.w[:, a:a + n]).then_inc(sem["lw%d" % i], 16)
+    act.dma_start(T.ml[:, :], T.mp[:, :]).then_inc(sem.lml, 16)
+    done["sl"], done["ml"] = ("lsl", SLP), ("lml", 16)
+    piece = []
+    for i, n in enumerate(PIECES):
+        k, o = TILE[len(piece)]
+        a, b = 512 * (k * O + o), 512 * len(piece)
+        g.sync.dma_start(T.wb[:, b:b + 512 * n], T.w[:, a:a + 512 * n]).then_inc(sem["lw%d" % i], 16)
         done["w%d" % i] = ("lw%d" % i, 16)
+        piece += [i] * n
 
     calls = {}
     lw = CAP // 16
@@ -100,22 +109,24 @@ def rank_program(g, core, T, topo):
     def slots(p, a, b, c):
         return lambda: vec.tensor_scalar(T.so[p:p + SLP, a:b], T.sl[0:SLP, c:c + b - a], 4.0, 0.0, AluOpType.mult, AluOpType.max)
 
-    runs = [(0, lw * r, 0), (lw * r, lw * (N - 1), lw * (r + 1))]
-    calls["so"] = [(["sl"], slots(p, *x)) for p in range(0, 128, SLP) for x in runs if x[1] > x[0]]
+    runs = []
+    for j, d in enumerate(peers):
+        if runs and runs[-1][2] + runs[-1][1] - runs[-1][0] == lw * d:
+            runs[-1][1] += lw
+        else:
+            runs.append([lw * j, lw * j + lw, lw * d])
+    calls["so"] = [(["sl"], slots(p, *x)) for x in runs for p in range(0, 128, SLP)]
     calls["zero"] = [([], lambda: vec.memset(T.win[:, 0:K * O * WS:WS], 0.0))]
     edge = float(TC + CAP * (r + 1))
+    calls["ma"] = [(["ml"], lambda: vec.tensor_scalar(T.mt[:], T.ml[:], edge, -float(CAP), AluOpType.is_ge, AluOpType.mult))]
+    calls["mb"] = [(["ma"], lambda: vec.tensor_tensor(T.mu[:], T.mt[:], T.ml[:], add))]
+    calls["mo"] = [(["mb"], lambda: vec.tensor_scalar(T.mv[:], T.mu[:], 1.0, None, add))]
 
-    def maps(p, src):
-        return lambda: vec.tensor_scalar(T.mo[p:p + MLP, :], src[0:MLP, :], 1.0, None, add)
-
-    if r == N - 1:
-        calls["ma"], calls["mb"] = [], []
-        done["ma"] = done["mb"] = done["ml"]
-        calls["mo"] = [(["ml"], maps(p, T.ml)) for p in range(0, 128, MLP)]
-    else:
-        calls["ma"] = [(["ml"], lambda: vec.tensor_scalar(T.mt[0:MLP, :], T.ml[0:MLP, :], edge, -float(CAP), AluOpType.is_ge, AluOpType.mult))]
-        calls["mb"] = [(["ma"], lambda: vec.tensor_tensor(T.mu[0:MLP, :], T.mt[0:MLP, :], T.ml[0:MLP, :], add))]
-        calls["mo"] = [(["mb"], maps(p, T.mu)) for p in range(0, 128, MLP)]
+    def spread():
+        wait("y", done["mo"])
+        for b in range(8):
+            g.sync.dma_start(T.mo[16 * b:16 * b + 16, :], T.mv[:, :]).then_inc(sem.lmo, 16)
+        done["maps"] = ("lmo", 128)
 
     def copy(name, out, src):
         if name in VECTOR:
@@ -125,14 +136,16 @@ def rank_program(g, core, T, topo):
     def quant(cq, cp, src, a, b):
         return lambda: vec.quantize_mx(cq[:, a:b], cp[:, a:b], src[:, 4 * a:4 * b])
 
-    for t in range(4):
-        name = "h%d" % t
-        calls[name] = [(["so", "x0", "x1"], copy(name, T.h[:, t:4 * FAR:4], T.xs[:, t:4 * TC].indirect(T.so[:, 0:FAR // 16])))]
-    calls["qh"] = [(["h0", "h1", "h2", "h3"], quant(T.hq, T.hs, T.h, 0, FAR))]
+    picks = [name for name in VECTOR + SCALAR if name[0] == "h"]
+    for name in picks:
+        t, (a, b) = int(name[1]), {"": (0, FAR), "a": (0, CAP), "b": (CAP, FAR)}[name[2:]]
+        calls[name] = [(["so", "x0", "x1"], copy(name, T.h[:, 4 * a + t:4 * b:4], T.xs[:, t:4 * TC].indirect(T.so[:, a // 16:b // 16])))]
+    calls["qha"] = [([p for p in picks if p[2:] != "b"], quant(T.hq, T.hs, T.h, 0, CAP))]
+    calls["qhb"] = [([p for p in picks if p[2:] != "a"], quant(T.hq, T.hs, T.h, CAP, FAR))]
     for i in range(2):
         calls["qx%d" % i] = [(["x%d" % i], quant(T.xq, T.xp, T.xs, TC // 2 * i, TC // 2 * (i + 1)))]
-    for i in range(K * O // PAIR):
-        calls["qw%d" % i] = [(["w%d" % i], quant(T.wq, T.wp, T.wb, 128 * PAIR * i, 128 * PAIR * (i + 1)))]
+    for i, n in enumerate(PIECES):
+        calls["qw%d" % i] = [(["w%d" % i], quant(T.wq, T.wp, T.wb, 128 * piece.index(i), 128 * (piece.index(i) + n)))]
 
     def product(i, q, p, n, bank):
         w = slice(128 * i, 128 * i + 128)
@@ -144,7 +157,7 @@ def rank_program(g, core, T, topo):
     for j, name in enumerate(TENSOR):
         far, i, bank = name[0] == "N", int(name[1:]), j % BANKS
         n, e = (FAR if far else TC), out_of(name)
-        need = (["arr"] if far else ["qx0", "qx1"]) + ["qw%d" % (i // PAIR)] + ([out_of(TENSOR[j - BANKS])] if j >= BANKS else [])
+        need = (["arr"] if far else ["qx0", "qx1"]) + ["qw%d" % piece[i]] + ([out_of(TENSOR[j - BANKS])] if j >= BANKS else [])
         calls[name] = [(need, product(i, T.fq if far else T.xq, T.fp if far else T.xp, n, bank))]
         a = WS * i + 1 + (TC if far else 0)
         calls[e] = [([name], copy(e, T.win[:, a:a + n], T.ps[:, 512 * bank:512 * bank + n]))]
@@ -153,52 +166,53 @@ def rank_program(g, core, T, topo):
         m = TILE[i][0] * (TC // 16)
         return T.win[:, WS * i:WS * i + WS].indirect(T.mo[:, m + a // 16:m + b // 16])
 
-    def more(i, a, b):
-        o = TILE[i][1]
-        at = T.acc[:, TC * o + a:TC * o + b]
+    def more(i, at, a, b):
         return lambda: vec.tensor_tensor(at, window(i, a, b), at, add)
 
     leave = []
-    for o in range(O):
-        tiles = [i for i in range(K * O) if TILE[i][1] == o]
-        first = [i for i in tiles if "I%d" % i in SCALAR + VECTOR][0]
+    for j, tiles in enumerate(SUMS):
+        first = tiles[0]
         last = "I%d" % first
-        calls[last] = [(["zero", "mo", "E%d" % first, "F%d" % first], copy(last, T.acc[:, TC * o:TC * o + TC], window(first, 0, TC)))]
-        rest = [i for i in tiles if i != first]
-        rest.sort(key=lambda i: VECTOR.index("G%d" % i if "G%d" % i in VECTOR else "G%da" % i))
-        for i in rest:
-            need = ["zero", "mo", "E%d" % i, "F%d" % i, last]
+        calls[last] = [(["zero", "maps", "E%d" % first, "F%d" % first], copy(last, T.acc[:, TC * j:TC * j + TC], window(first, 0, TC)))]
+        for i in tiles[1:]:
+            need = ["zero", "maps", "E%d" % i, "F%d" % i, last]
             last = "G%d" % i
-            parts = [(last, 0, TC)] if last in VECTOR else [(last + "abc"[j], a, b) for j, (a, b) in enumerate(LAST)]
+            parts = [(last, 0, TC)] if last in VECTOR else [(last + "abc"[p], a, b) for p, (a, b) in enumerate(LAST)]
             for name, a, b in parts:
-                calls[name] = [(need, more(i, a, b))]
-        leave += [(name, TC * o + a, TC * o + b) for name, a, b in parts]
+                calls[name] = [(need, more(i, T.acc[:, TC * j + a:TC * j + b], a, b))]
+        leave += [(name, TILE[first][1], a, b, T.acc[:, TC * j + a:TC * j + b]) for name, a, b in parts]
     leave.sort(key=lambda x: VECTOR.index(x[0]))
 
     width = {d: engines_for(topo, cores, core, cores[d]) for d in peers}
     done["arr"] = ("arr", sum(2 * len(engines_for(topo, cores, cores[s], core)) for s in peers))
 
-    def send():
-        wait("g", done["qh"])
-        for codes in (True, False):
-            transfers = []
-            for d in peers:
-                rid, pid = topo.addr(cores[d])[:2]
-                a, b = CAP * place(r, d), CAP * place(d, r)
-                if codes:
-                    src, dst = T.hq[:, a:a + CAP].bitcast(dt.uint8), T.fq[:, b:b + CAP].bitcast(dt.uint8)
-                else:
-                    src, dst = T.hs[:, a:a + CAP], T.fp[:, b:b + CAP]
-                transfers.append(RemoteDMATransfer(dst_ids=[DstId(rid=rid, pnc=pid)], dma_engine_mask=sum(1 << e for e in width[d]),
-                                                   remote_sem=sem.arr, src=src, dst=dst))
-            g.remote_dma_fused(transfers, local_sem=sem.loc)
+    def send(to, codes):
+        transfers = []
+        for d in to:
+            rid, pid = topo.addr(cores[d])[:2]
+            a, b = CAP * place(r, d), CAP * place(d, r)
+            if codes:
+                src, dst = T.hq[:, a:a + CAP].bitcast(dt.uint8), T.fq[:, b:b + CAP].bitcast(dt.uint8)
+            else:
+                src, dst = T.hs[:, a:a + CAP], T.fp[:, b:b + CAP]
+            transfers.append(RemoteDMATransfer(dst_ids=[DstId(rid=rid, pnc=pid)], dma_engine_mask=sum(1 << e for e in width[d]),
+                                               remote_sem=sem.arr, src=src, dst=dst))
+        g.remote_dma_fused(transfers, local_sem=sem.loc)
+
+    def after(name):
+        if name == "mo":
+            spread()
+        if name == "qhb":
+            wait("g", done["qhb"])
+            send(peers, True)
+            send(peers, False)
 
     orders = {"v": list(VECTOR), "s": list(SCALAR), "p": list(TENSOR)}
     moved = True
     while moved:
         moved = False
         for q in orders:
-            while orders[q] and all(d in done or d == orders[q][0] for need, c in calls[orders[q][0]] for d in need):
+            while orders[q] and all(d in done for need, c in calls[orders[q][0]] for d in need):
                 name = orders[q].pop(0)
                 for need, call in calls[name]:
                     for d in need:
@@ -206,16 +220,25 @@ def rank_program(g, core, T, topo):
                     call().then_inc(sem[q], 1)
                     count[q] += 1
                     done[name] = (q, count[q])
-                if name == "qh":
-                    send()
+                after(name)
                 moved = True
     if any(orders.values()):
         raise ValueError("no order: %s" % orders)
 
-    for name, a, b in leave:
-        wait("y", done[name])
-        g.sync.dma_start(T.y[:, a:b], T.acc[:, a:b]).then_inc(sem.ly, 16)
+    stored = {}
+    for name, o, a, b, src in leave:
+        out, own = T.y[:, TC * o + a:TC * o + b], "ly%d" % o
+        if o in TWICE and own in stored:
+            wait("g", done[name])
+            wait("g", (own, stored[own]))
+            g.dma_start(out, src, accum_op=add).then_inc(sem.lg, 16)
+            stored["lg"] = stored.get("lg", 0) + 16
+        else:
+            wait("y", done[name])
+            g.sync.dma_start(out, src).then_inc(sem[own], 16)
+            stored[own] = stored.get(own, 0) + 16
     g.wait_ge(sem.loc, 2 * sum(len(width[d]) for d in peers))
     for q in orders:
         wait("y", (q, count[q]))
-    g.sync.wait_ge(sem.ly, 16 * len(leave))
+    for name in stored:
+        wait("g" if name == "lg" else "y", (name, stored[name]))

from concourse.bass import DstId, RemoteDMATransfer
from concourse.mybir import dt, AluOpType, ActivationFunctionType

N, TC, K, O, CAP = 4, 512, 4, 4, 128
FAR = (N - 1) * CAP
WS = 1 + TC + FAR
PAIR = 2
PIECES = [1, 1] + [PAIR] * 7
BANKS = 8
LAST = [(0, 192), (192, 384), (384, 512)]
TILE = [(k, o) for h in range(0, O, PAIR) for k in range(K) for o in range(h, h + PAIR)]
SUMS = [[0, 2], [4, 6], [1, 3], [5, 7], [8, 10, 12, 14], [9, 11, 13, 15]]
TWICE = [o for o in range(O) if [TILE[s[0]][1] for s in SUMS].count(o) > 1]
SLP = 32
MP = 32
MW = K * TC // MP
NEAR = 4

SCRATCH = {
    "xs": ("sbuf", [128, 4 * TC], "bfloat16"),
    "wb": ("sbuf", [128, 512 * K * O], "bfloat16"),
    "sl": ("sbuf", [128, N * CAP // 16], "int32"),
    "ml": ("sbuf", [MP, MW], "int32"),
    "mt": ("sbuf", [MP, MW], "int32"),
    "mu": ("sbuf", [MP, MW], "int32"),
    "mv": ("sbuf", [MP, MW], "uint16"),
    "so": ("sbuf", [128, FAR // 16], "uint16"),
    "mo": ("sbuf", [128, K * TC // 16], "uint16"),
    "h": ("sbuf", [128, 4 * FAR], "bfloat16"),
    "hq": ("sbuf", [128, FAR], "float8_e4m3fn_x4"),
    "hs": ("sbuf", [128, FAR], "uint8"),
    "xq": ("sbuf", [128, TC], "float8_e4m3fn_x4"),
    "xp": ("sbuf", [128, TC], "uint8"),
    "wq": ("sbuf", [128, 128 * K * O], "float8_e4m3fn_x4"),
    "wp": ("sbuf", [128, 128 * K * O], "uint8"),
    "fq": ("sbuf", [128, FAR], "float8_e4m3fn_x4"),
    "fp": ("sbuf", [128, FAR], "uint8"),
    "win": ("sbuf", [128, K * O * WS], "float32"),
    "acc": ("sbuf", [128, len(SUMS) * TC], "float32"),
    "ps": ("psum", [128, 512 * BANKS], "float32"),
}
SEMAPHORES = ["v", "s", "p", "arr", "loc", "lsl", "lml", "lmo", "lx0", "lx1", "lg"] + ["ly%d" % o for o in range(O)] + ["lw%d" % i for i in range(len(PIECES))]

VECTOR = """zero so qx0 qx1 qw0 h0 qw1 h1a qw2 qha qhb qw3 ma qw4 mb qw5 mo E4 qw6 qw7 E7 qw8 E10 E12 E13
    F0 F2 F3 F4 G2 F6 G3 F10 G6 F7 G10 G7 G12 G11 G14 G13 G15a G15b G15c""".split()
SCALAR = """h2 h3 h1b E0 E1 E2 E3 E5 E6 E8 E9 E11 E14
    F1 I0 I1 F8 I4 F5 I8 I5 F9 F12 F11 I9 F14 F13 F15 E15""".split()
TENSOR = """M0 M1 M2 M3 M4 M5 M6 M7 M8 M9 M10 M11 M12 M13 M14
    N0 N1 N2 N3 N4 N8 N6 N5 N10 N7 N9 N12 N11 N14 N13 N15 M15""".split()


def place(at, other):
    return other if other < at else other - 1


def engines_for(topo, cores, src, dst):
    peers = [c for c in cores if c != src]
    out = [c for c in peers if topo.chip(c) != topo.chip(src)]
    if dst in out:
        e = topo.engines(src, dst)
        n = len(e) // len(out)
        i = out.index(dst)
        return e[i * n:(i + 1) * n]
    used = {e for c in out for e in topo.engines(src, c)}
    free = [e for e in topo.engines(src, dst) if e not in used]
    return free[::len(free) // NEAR]


def rank_program(g, core, T, topo):
    r = T.rank_of(core)
    if r is None:
        return
    cores = list(T.cores)
    sem = T.sem
    peers = [d for d in range(N) if d != r]
    vec, act = g.vector, g.scalar
    Copy = ActivationFunctionType.Copy
    add = AluOpType.add
    queue = {"v": g.vector, "s": g.scalar, "p": g.tensor, "y": g.sync, "g": g}
    count = {"v": 0, "s": 0, "p": 0}
    done = {}
    waited = {}

    def wait(q, token):
        name, val = token
        if waited.get((q, name), 0) < val:
            queue[q].wait_ge(sem[name], val)
            waited[(q, name)] = val

    for b, q in enumerate((act, g.sync) * (SLP // 32)):
        q.dma_start(T.sl[16 * b:16 * b + 16, :], T.send[:, :]).then_inc(sem.lsl, 16)
    half = 2 * TC
    for i in range(2):
        g.sync.dma_start(T.xs[:, half * i:half * i + half], T.x[:, half * i:half * i + half]).then_inc(sem["lx%d" % i], 16)
        done["x%d" % i] = ("lx%d" % i, 16)
    act.dma_start(T.ml[:, :], T.mp[:, :]).then_inc(sem.lml, 16)
    done["sl"], done["ml"] = ("lsl", SLP), ("lml", 16)
    piece = []
    for i, n in enumerate(PIECES):
        k, o = TILE[len(piece)]
        a, b = 512 * (k * O + o), 512 * len(piece)
        g.sync.dma_start(T.wb[:, b:b + 512 * n], T.w[:, a:a + 512 * n]).then_inc(sem["lw%d" % i], 16)
        done["w%d" % i] = ("lw%d" % i, 16)
        piece += [i] * n

    calls = {}
    lw = CAP // 16

    def slots(p, a, b, c):
        return lambda: vec.tensor_scalar(T.so[p:p + SLP, a:b], T.sl[0:SLP, c:c + b - a], 4.0, 0.0, AluOpType.mult, AluOpType.max)

    runs = []
    for j, d in enumerate(peers):
        if runs and runs[-1][2] + runs[-1][1] - runs[-1][0] == lw * d:
            runs[-1][1] += lw
        else:
            runs.append([lw * j, lw * j + lw, lw * d])
    calls["so"] = [(["sl"], slots(p, *x)) for x in runs for p in range(0, 128, SLP)]
    calls["zero"] = [([], lambda: vec.memset(T.win[:, 0:K * O * WS:WS], 0.0))]
    edge = float(TC + CAP * (r + 1))
    calls["ma"] = [(["ml"], lambda: vec.tensor_scalar(T.mt[:], T.ml[:], edge, -float(CAP), AluOpType.is_ge, AluOpType.mult))]
    calls["mb"] = [(["ma"], lambda: vec.tensor_tensor(T.mu[:], T.mt[:], T.ml[:], add))]
    calls["mo"] = [(["mb"], lambda: vec.tensor_scalar(T.mv[:], T.mu[:], 1.0, None, add))]

    def spread():
        wait("y", done["mo"])
        for b in range(8):
            g.sync.dma_start(T.mo[16 * b:16 * b + 16, :], T.mv[:, :]).then_inc(sem.lmo, 16)
        done["maps"] = ("lmo", 128)

    def copy(name, out, src):
        if name in VECTOR:
            return lambda: vec.tensor_copy(out, src)
        return lambda: act.activation(out, src, Copy)

    def quant(cq, cp, src, a, b):
        return lambda: vec.quantize_mx(cq[:, a:b], cp[:, a:b], src[:, 4 * a:4 * b])

    picks = [name for name in VECTOR + SCALAR if name[0] == "h"]
    for name in picks:
        t, (a, b) = int(name[1]), {"": (0, FAR), "a": (0, CAP), "b": (CAP, FAR)}[name[2:]]
        calls[name] = [(["so", "x0", "x1"], copy(name, T.h[:, 4 * a + t:4 * b:4], T.xs[:, t:4 * TC].indirect(T.so[:, a // 16:b // 16])))]
    calls["qha"] = [([p for p in picks if p[2:] != "b"], quant(T.hq, T.hs, T.h, 0, CAP))]
    calls["qhb"] = [([p for p in picks if p[2:] != "a"], quant(T.hq, T.hs, T.h, CAP, FAR))]
    for i in range(2):
        calls["qx%d" % i] = [(["x%d" % i], quant(T.xq, T.xp, T.xs, TC // 2 * i, TC // 2 * (i + 1)))]
    for i, n in enumerate(PIECES):
        calls["qw%d" % i] = [(["w%d" % i], quant(T.wq, T.wp, T.wb, 128 * piece.index(i), 128 * (piece.index(i) + n)))]

    def product(i, q, p, n, bank):
        w = slice(128 * i, 128 * i + 128)
        return lambda: g.tensor.matmul_mx(T.ps[:, 512 * bank:512 * bank + n], T.wq[:, w], T.wp[:, w], q[:, 0:n], p[:, 0:n], True, True)

    def out_of(name):
        return {"M": "E", "N": "F"}[name[0]] + name[1:]

    for j, name in enumerate(TENSOR):
        far, i, bank = name[0] == "N", int(name[1:]), j % BANKS
        n, e = (FAR if far else TC), out_of(name)
        need = (["arr"] if far else ["qx0", "qx1"]) + ["qw%d" % piece[i]] + ([out_of(TENSOR[j - BANKS])] if j >= BANKS else [])
        calls[name] = [(need, product(i, T.fq if far else T.xq, T.fp if far else T.xp, n, bank))]
        a = WS * i + 1 + (TC if far else 0)
        calls[e] = [([name], copy(e, T.win[:, a:a + n], T.ps[:, 512 * bank:512 * bank + n]))]

    def window(i, a, b):
        m = TILE[i][0] * (TC // 16)
        return T.win[:, WS * i:WS * i + WS].indirect(T.mo[:, m + a // 16:m + b // 16])

    def more(i, at, a, b):
        return lambda: vec.tensor_tensor(at, window(i, a, b), at, add)

    leave = []
    for j, tiles in enumerate(SUMS):
        first = tiles[0]
        last = "I%d" % first
        calls[last] = [(["zero", "maps", "E%d" % first, "F%d" % first], copy(last, T.acc[:, TC * j:TC * j + TC], window(first, 0, TC)))]
        for i in tiles[1:]:
            need = ["zero", "maps", "E%d" % i, "F%d" % i, last]
            last = "G%d" % i
            parts = [(last, 0, TC)] if last in VECTOR else [(last + "abc"[p], a, b) for p, (a, b) in enumerate(LAST)]
            for name, a, b in parts:
                calls[name] = [(need, more(i, T.acc[:, TC * j + a:TC * j + b], a, b))]
        leave += [(name, TILE[first][1], a, b, T.acc[:, TC * j + a:TC * j + b]) for name, a, b in parts]
    leave.sort(key=lambda x: VECTOR.index(x[0]))

    width = {d: engines_for(topo, cores, core, cores[d]) for d in peers}
    done["arr"] = ("arr", sum(2 * len(engines_for(topo, cores, cores[s], core)) for s in peers))

    def send(to, codes):
        transfers = []
        for d in to:
            rid, pid = topo.addr(cores[d])[:2]
            a, b = CAP * place(r, d), CAP * place(d, r)
            if codes:
                src, dst = T.hq[:, a:a + CAP].bitcast(dt.uint8), T.fq[:, b:b + CAP].bitcast(dt.uint8)
            else:
                src, dst = T.hs[:, a:a + CAP], T.fp[:, b:b + CAP]
            transfers.append(RemoteDMATransfer(dst_ids=[DstId(rid=rid, pnc=pid)], dma_engine_mask=sum(1 << e for e in width[d]),
                                               remote_sem=sem.arr, src=src, dst=dst))
        g.remote_dma_fused(transfers, local_sem=sem.loc)

    def after(name):
        if name == "mo":
            spread()
        if name == "qhb":
            wait("g", done["qhb"])
            send(peers, True)
            send(peers, False)

    orders = {"v": list(VECTOR), "s": list(SCALAR), "p": list(TENSOR)}
    moved = True
    while moved:
        moved = False
        for q in orders:
            while orders[q] and all(d in done for need, c in calls[orders[q][0]] for d in need):
                name = orders[q].pop(0)
                for need, call in calls[name]:
                    for d in need:
                        wait(q, done[d])
                    call().then_inc(sem[q], 1)
                    count[q] += 1
                    done[name] = (q, count[q])
                after(name)
                moved = True
    if any(orders.values()):
        raise ValueError("no order: %s" % orders)

    stored = {}
    for name, o, a, b, src in leave:
        out, own = T.y[:, TC * o + a:TC * o + b], "ly%d" % o
        if o in TWICE and own in stored:
            wait("g", done[name])
            wait("g", (own, stored[own]))
            g.dma_start(out, src, accum_op=add).then_inc(sem.lg, 16)
            stored["lg"] = stored.get("lg", 0) + 16
        else:
            wait("y", done[name])
            g.sync.dma_start(out, src).then_inc(sem[own], 16)
            stored[own] = stored.get(own, 0) + 16
    g.wait_ge(sem.loc, 2 * sum(len(width[d]) for d in peers))
    for q in orders:
        wait("y", (q, count[q]))
    for name in stored:
        wait("g" if name == "lg" else "y", (name, stored[name]))
